import numpy as np
import ml_dtypes


def mxq(x, axis, fmt="e4m3"):
    dtype, down = {"e4m3": (ml_dtypes.float8_e4m3fn, 7), "e5m2": (ml_dtypes.float8_e5m2, 14)}[fmt]
    v = np.moveaxis(np.asarray(x, np.float32).astype(ml_dtypes.bfloat16).astype(np.float64), axis, -1)
    blocks = v.reshape(v.shape[:-1] + (-1, 32))
    amax = np.abs(blocks).max(-1, keepdims=True)
    byte = np.maximum(np.where(amax > 0, np.frexp(amax)[1] - 1 + 127, 0) - down, 1)
    scale = np.exp2(byte - 127.0)
    codes = (blocks / scale).astype(np.float32).astype(dtype).astype(np.float64)
    return np.moveaxis((codes * scale).reshape(v.shape), -1, axis)


WIDE = False


def mx_kscale(k):
    if not WIDE:
        return np.ones(k)
    levels = np.array([10, -10, 5, -5, 0])
    if k % 512:
        return np.exp2(np.random.permutation(np.resize(levels, k // 32))).repeat(32)
    a = np.empty((k // 512, 16))
    for p in range(k // 512):
        a[p, :8] = np.random.permutation(np.resize(levels, 8))
        for g in range(8):
            far = levels[np.abs(levels - a[p, g]) >= 10]
            a[p, g + 8] = far[np.random.randint(len(far))]
    return np.exp2(a.ravel()).repeat(32)


def f64(x):
    return np.asarray(x).astype(np.float64)


def striped(idx):
    return np.tile(idx.reshape(-1, 16).T, (8, 1)).astype(np.uint16)


def unstriped(offs):
    return offs[:16].T.reshape(-1).astype(np.int64)


def pack_weight(w):
    k, n = w.shape
    w = f64(np.asarray(w, np.float32).astype(ml_dtypes.bfloat16)).reshape(k // 32, 32, n)
    amax = np.abs(w).max(1)
    byte = np.clip(np.where(amax > 0, np.frexp(amax)[1] - 1 + 127 - 7, 1), 1, 254)
    scaled = (w * np.exp2(127.0 - byte)[:, None, :]).reshape(k, n).astype(np.float32)
    words = np.ascontiguousarray(scaled.reshape(k // 512, 128, 4, n).transpose(0, 1, 3, 2)).astype(ml_dtypes.float8_e4m3fn).view(np.uint8)
    return words, np.ascontiguousarray(byte.astype(np.uint8).reshape(k // 512, 16, n))


def unpack_weight(words, scales):
    g, p, n, _ = words.shape
    vals = np.ascontiguousarray(words).view(ml_dtypes.float8_e4m3fn).astype(np.float64) * np.repeat(np.exp2(scales.astype(np.float64) - 127.0), 8, axis=1)[..., None]
    return vals.transpose(0, 1, 3, 2).reshape(g * 512, n)


def relu(v):
    return np.maximum(v, 0.0)


K, T, D, S, V, N = 512, 1024, 6, 3072, 512, 128


def setup_inputs():
    n = np.random.standard_normal
    s = mx_kscale(K)[:, None]
    words, scales = pack_weight(n((K, N)) / np.sqrt(K) / s)
    return {
        "xT": (n((K, T)) * s).astype(np.float32),
        "w_words": words,
        "w_scales": scales,
        "b": (0.3 * n((N, 1))).astype(np.float32),
        "gate": np.tile(np.random.uniform(0.2, 1.0, (D, 1, V)) / np.sqrt(D), (1, N, 1)).astype(np.float32),
        "pos1": striped(np.random.permutation(T)[:V]),
        "pos2": striped(np.random.permutation(T)[:V]),
        "pos3": striped(np.random.permutation(T)[:V]),
        "pos4": striped(np.random.permutation(T)[:V]),
        "pos5": striped(np.random.permutation(T)[:V]),
        "pos6": striped(np.random.permutation(T)[:V]),
    }


def reference(xT, w_words, w_scales, b, gate, pos1, pos2, pos3, pos4, pos5, pos6):
    w = unpack_weight(w_words, w_scales)
    y = w.T @ mxq(f64(xT), 0, "e4m3")
    y = relu(y + f64(b))
    return sum(f64(gate[d]) * y[:, unstriped(p)] for d, p in enumerate((pos1, pos2, pos3, pos4, pos5, pos6)))

@@ -1,0 +1,131 @@
+from contextlib import ExitStack
+
+import concourse.mybir as mybir
+
+K, T, D, V, N = 512, 1024, 6, 512, 128
+P = 128
+PACK = 4
+FLOPS = 2 * K * N * T + 2 * D * N * V
+
+F32 = mybir.dt.float32
+BF16 = mybir.dt.bfloat16
+I32 = mybir.dt.int32
+U32 = mybir.dt.uint32
+U16 = mybir.dt.uint16
+U8 = mybir.dt.uint8
+FP8X4 = mybir.dt.float8_e4m3fn_x4
+RELU = mybir.ActivationFunctionType.Relu
+MULT = mybir.AluOpType.mult
+ADD = mybir.AluOpType.add
+
+CHUNKS = ((512, 320), (256, 160), (128, 64), (128, 64))
+HALF = V // 2
+
+
+def tile_picked_agg_lin_relu_sub_l_kernel(
+    tc, xT, w_words, w_scales, b, gate, pos1, pos2, pos3, pos4, pos5, pos6, out
+):
+    nc = tc.nc
+    with ExitStack() as ctx:
+        lists = ctx.enter_context(tc.tile_pool(name="lists", bufs=1))
+        keep = ctx.enter_context(tc.tile_pool(name="keep", bufs=1))
+        psum = ctx.enter_context(tc.psum_pool(name="psum", bufs=1))
+
+        offsets = [lists.tile([P, V // 16], U16, name=f"offsets{d}") for d in range(D)]
+
+        w_plane = keep.tile([P, N], U8, align_bytes=64)
+        nc.vector.memset(w_plane[:].bitcast(I32), 0)
+        warm = keep.tile([P, 8], F32)
+        nc.vector.memset(warm[:], 0.0)
+
+        w_codes = keep.tile([P, N * PACK], U8, align_bytes=64)
+        nc.scalar.dma_start(out=w_codes[:].bitcast(I32), in_=w_words.rearrange("a p m r -> (a p) (m r)").bitcast(I32))
+        bias = keep.tile([P, 1], F32)
+        nc.scalar.dma_start(out=bias[:], in_=b)
+        scale_rows = w_scales.rearrange("a q m -> (a q) m")
+        for q in range(4):
+            nc.scalar.dma_start(
+                out=w_plane[32 * q : 32 * q + 4, :].bitcast(I32), in_=scale_rows[4 * q : 4 * q + 4, :].bitcast(I32)
+            )
+        warm_out = keep.tile([P, 8], F32)
+        nc.scalar.activation(warm_out[:], warm[:], RELU)
+
+        x_rows = xT.rearrange("(p j) t -> p j t", j=PACK)
+        raws = []
+        first = 0
+        for c, (nodes, _) in enumerate(CHUNKS):
+            raw = keep.tile([P, PACK, nodes], F32, name=f"raw{c}")
+            nc.sync.dma_start(out=raw[:], in_=x_rows[:, :, first : first + nodes])
+            raws.append(raw)
+            first += nodes
+
+        gates = [keep.tile([P, d1 - d0, V], F32, name=f"gates{d0}") for d0, d1 in ((0, 1), (1, 3), (3, 6))]
+        positions = (pos1, pos2, pos3, pos4, pos5, pos6)
+
+        def load_list(d):
+            nc.sync.dma_start(out=offsets[d][:], in_=positions[d])
+
+        def load_gates(g, d0, d1):
+            nc.sync.dma_start(out=gates[g][:], in_=gate[d0:d1].rearrange("d p v -> p d v"))
+
+        load_list(0)
+        load_gates(0, 0, 1)
+        load_list(1)
+        load_list(2)
+        load_gates(1, 1, 3)
+        load_list(3)
+        load_list(4)
+        load_list(5)
+        load_gates(2, 3, 6)
+
+        y = keep.tile([P, T], F32)
+        first = 0
+        for c, (nodes, by_vector) in enumerate(CHUNKS):
+            grouped = keep.tile([P, nodes, PACK], BF16, align_bytes=64, name=f"grouped{c}")
+            stepped = raws[c][:].rearrange("p j t -> p t j")
+            nc.vector.tensor_copy(grouped[:, :by_vector, :], stepped[:, :by_vector, :])
+            nc.scalar.copy(grouped[:, by_vector:, :], stepped[:, by_vector:, :])
+            codes = keep.tile([P, nodes], U32, align_bytes=64, name=f"codes{c}")
+            plane = keep.tile([P, nodes], U8, align_bytes=64, name=f"plane{c}")
+            nc.vector.quantize_mx(
+                out=codes[:].bitcast(FP8X4), scales=plane[:], in_=grouped[:].rearrange("p t j -> p (t j)")
+            )
+            acc = psum.tile([P, nodes], F32, name=f"acc{c}")
+            nc.tensor.matmul_mx(
+                out=acc[:],
+                lhsT=w_codes[:].bitcast(FP8X4),
+                lhsT_scale=w_plane[:],
+                rhs=codes[:].bitcast(FP8X4),
+                rhs_scale=plane[:],
+                start=True,
+                stop=True,
+            )
+            nc.scalar.activation(y[:, first : first + nodes], acc[:], RELU, bias=bias[:])
+            first += nodes
+
+        gate_of = [gates[0][:, 0, :], gates[1][:, 0, :], gates[1][:, 1, :]] + [gates[2][:, d, :] for d in range(3)]
+        terms = [keep.tile([P, V], F32, name=f"term{d}") for d in range(D)]
+        sums = [keep.tile([P, V], F32, name=f"sum{d}") for d in range(5)]
+
+        def neighbour(d, v0=0, v1=V):
+            idx = offsets[d][:, v0 // 16 : v1 // 16]
+            nc.vector.tensor_tensor(terms[d][:, v0:v1], y[:].indirect(idx), gate_of[d][:, v0:v1], MULT)
+
+        def add(dst, a, b_, v0=0, v1=V):
+            nc.vector.tensor_tensor(dst[:, v0:v1], a[:, v0:v1], b_[:, v0:v1], ADD)
+
+        neighbour(0)
+        neighbour(1)
+        neighbour(2)
+        add(sums[0], terms[0], terms[1])
+        neighbour(3)
+        add(sums[1], sums[0], terms[2])
+        neighbour(4)
+        add(sums[2], sums[1], terms[3])
+        neighbour(5, 0, HALF)
+        add(sums[3], sums[2], terms[4])
+        neighbour(5, HALF, V)
+        add(sums[4], sums[3], terms[5], 0, HALF)
+        nc.sync.dma_start(out=out[:, 0:HALF], in_=sums[4][:, 0:HALF])
+        add(sums[4], sums[3], terms[5], HALF, V)
+        nc.sync.dma_start(out=out[:, HALF:V], in_=sums[4][:, HALF:V])

@@ -18,7 +18,7 @@ RELU = mybir.ActivationFunctionType.Relu
 MULT = mybir.AluOpType.mult
 ADD = mybir.AluOpType.add
 
-CHUNKS = ((512, 320), (256, 160), (128, 64), (128, 64))
+CHUNKS = ((256, 160), (256, 160), (256, 160), (128, 80), (128, 64))
 HALF = V // 2
 
 

@@ -18,7 +18,7 @@ RELU = mybir.ActivationFunctionType.Relu
 MULT = mybir.AluOpType.mult
 ADD = mybir.AluOpType.add
 
-CHUNKS = ((256, 160), (256, 160), (256, 160), (128, 80), (128, 64))
+LOADS = ((0, 512), (512, 832), (832, 1024))
 HALF = V // 2
 
 
@@ -52,12 +52,10 @@ def tile_picked_agg_lin_relu_sub_l_kernel(
 
         x_rows = xT.rearrange("(p j) t -> p j t", j=PACK)
         raws = []
-        first = 0
-        for c, (nodes, _) in enumerate(CHUNKS):
-            raw = keep.tile([P, PACK, nodes], F32, name=f"raw{c}")
-            nc.sync.dma_start(out=raw[:], in_=x_rows[:, :, first : first + nodes])
+        for c, (t0, t1) in enumerate(LOADS):
+            raw = keep.tile([P, PACK, t1 - t0], F32, name=f"raw{c}")
+            nc.sync.dma_start(out=raw[:], in_=x_rows[:, :, t0:t1])
             raws.append(raw)
-            first += nodes
 
         gates = [keep.tile([P, d1 - d0, V], F32, name=f"gates{d0}") for d0, d1 in ((0, 1), (1, 3), (3, 6))]
         positions = (pos1, pos2, pos3, pos4, pos5, pos6)
@@ -78,30 +76,61 @@ def tile_picked_agg_lin_relu_sub_l_kernel(
         load_list(5)
         load_gates(2, 3, 6)
 
+        grouped = keep.tile([P, T, PACK], BF16, align_bytes=64)
+        codes = keep.tile([P, T], U32, align_bytes=64)
+        planes = keep.tile([P, T], U8, align_bytes=64)
         y = keep.tile([P, T], F32)
-        first = 0
-        for c, (nodes, by_vector) in enumerate(CHUNKS):
-            grouped = keep.tile([P, nodes, PACK], BF16, align_bytes=64, name=f"grouped{c}")
-            stepped = raws[c][:].rearrange("p j t -> p t j")
-            nc.vector.tensor_copy(grouped[:, :by_vector, :], stepped[:, :by_vector, :])
-            nc.scalar.copy(grouped[:, by_vector:, :], stepped[:, by_vector:, :])
-            codes = keep.tile([P, nodes], U32, align_bytes=64, name=f"codes{c}")
-            plane = keep.tile([P, nodes], U8, align_bytes=64, name=f"plane{c}")
+        banks = {}
+
+        def loaded(t0, t1):
+            for raw, (l0, l1) in zip(raws, LOADS):
+                if l0 <= t0 and t1 <= l1:
+                    return raw[:, :, t0 - l0 : t1 - l0].rearrange("p j t -> p t j")
+
+        def by_vector(t0, t1):
+            nc.vector.tensor_copy(grouped[:, t0:t1, :], loaded(t0, t1))
+
+        def by_scalar(t0, t1):
+            nc.scalar.copy(grouped[:, t0:t1, :], loaded(t0, t1))
+
+        def project(t0, t1):
             nc.vector.quantize_mx(
-                out=codes[:].bitcast(FP8X4), scales=plane[:], in_=grouped[:].rearrange("p t j -> p (t j)")
+                out=codes[:, t0:t1].bitcast(FP8X4),
+                scales=planes[:, t0:t1],
+                in_=grouped[:, t0:t1, :].rearrange("p t j -> p (t j)"),
             )
-            acc = psum.tile([P, nodes], F32, name=f"acc{c}")
+            acc = psum.tile([P, t1 - t0], F32, name=f"acc{t0}")
             nc.tensor.matmul_mx(
                 out=acc[:],
                 lhsT=w_codes[:].bitcast(FP8X4),
                 lhsT_scale=w_plane[:],
-                rhs=codes[:].bitcast(FP8X4),
-                rhs_scale=plane[:],
+                rhs=codes[:, t0:t1].bitcast(FP8X4),
+                rhs_scale=planes[:, t0:t1],
                 start=True,
                 stop=True,
             )
-            nc.scalar.activation(y[:, first : first + nodes], acc[:], RELU, bias=bias[:])
-            first += nodes
+            banks[t0] = acc
+
+        def finish(t0, t1):
+            nc.scalar.activation(y[:, t0:t1], banks[t0][:], RELU, bias=bias[:])
+
+        by_vector(0, 304)
+        by_scalar(304, 512)
+        project(0, 256)
+        project(256, 512)
+        by_vector(512, 704)
+        by_scalar(704, 768)
+        finish(0, 256)
+        by_vector(768, 832)
+        project(512, 768)
+        finish(256, 512)
+        by_vector(832, 912)
+        by_scalar(912, 1024)
+        project(768, 896)
+        project(896, 1024)
+        finish(512, 768)
+        finish(768, 896)
+        finish(896, 1024)
 
         gate_of = [gates[0][:, 0, :], gates[1][:, 0, :], gates[1][:, 1, :]] + [gates[2][:, d, :] for d in range(3)]
         terms = [keep.tile([P, V], F32, name=f"term{d}") for d in range(D)]

from contextlib import ExitStack

import concourse.mybir as mybir

K, T, D, V, N = 512, 1024, 6, 512, 128
P = 128
PACK = 4
FLOPS = 2 * K * N * T + 2 * D * N * V

F32 = mybir.dt.float32
BF16 = mybir.dt.bfloat16
I32 = mybir.dt.int32
U32 = mybir.dt.uint32
U16 = mybir.dt.uint16
U8 = mybir.dt.uint8
FP8X4 = mybir.dt.float8_e4m3fn_x4
RELU = mybir.ActivationFunctionType.Relu
MULT = mybir.AluOpType.mult
ADD = mybir.AluOpType.add

LOADS = ((0, 512), (512, 832), (832, 1024))
HALF = V // 2


def tile_picked_agg_lin_relu_sub_l_kernel(
    tc, xT, w_words, w_scales, b, gate, pos1, pos2, pos3, pos4, pos5, pos6, out
):
    nc = tc.nc
    with ExitStack() as ctx:
        lists = ctx.enter_context(tc.tile_pool(name="lists", bufs=1))
        keep = ctx.enter_context(tc.tile_pool(name="keep", bufs=1))
        psum = ctx.enter_context(tc.psum_pool(name="psum", bufs=1))

        offsets = [lists.tile([P, V // 16], U16, name=f"offsets{d}") for d in range(D)]

        w_plane = keep.tile([P, N], U8, align_bytes=64)
        nc.vector.memset(w_plane[:].bitcast(I32), 0)
        warm = keep.tile([P, 8], F32)
        nc.vector.memset(warm[:], 0.0)

        w_codes = keep.tile([P, N * PACK], U8, align_bytes=64)
        nc.scalar.dma_start(out=w_codes[:].bitcast(I32), in_=w_words.rearrange("a p m r -> (a p) (m r)").bitcast(I32))
        bias = keep.tile([P, 1], F32)
        nc.scalar.dma_start(out=bias[:], in_=b)
        scale_rows = w_scales.rearrange("a q m -> (a q) m")
        for q in range(4):
            nc.scalar.dma_start(
                out=w_plane[32 * q : 32 * q + 4, :].bitcast(I32), in_=scale_rows[4 * q : 4 * q + 4, :].bitcast(I32)
            )
        warm_out = keep.tile([P, 8], F32)
        nc.scalar.activation(warm_out[:], warm[:], RELU)

        x_rows = xT.rearrange("(p j) t -> p j t", j=PACK)
        raws = []
        for c, (t0, t1) in enumerate(LOADS):
            raw = keep.tile([P, PACK, t1 - t0], F32, name=f"raw{c}")
            nc.sync.dma_start(out=raw[:], in_=x_rows[:, :, t0:t1])
            raws.append(raw)

        gates = [keep.tile([P, d1 - d0, V], F32, name=f"gates{d0}") for d0, d1 in ((0, 1), (1, 3), (3, 6))]
        positions = (pos1, pos2, pos3, pos4, pos5, pos6)

        def load_list(d):
            nc.sync.dma_start(out=offsets[d][:], in_=positions[d])

        def load_gates(g, d0, d1):
            nc.sync.dma_start(out=gates[g][:], in_=gate[d0:d1].rearrange("d p v -> p d v"))

        load_list(0)
        load_gates(0, 0, 1)
        load_list(1)
        load_list(2)
        load_gates(1, 1, 3)
        load_list(3)
        load_list(4)
        load_list(5)
        load_gates(2, 3, 6)

        grouped = keep.tile([P, T, PACK], BF16, align_bytes=64)
        codes = keep.tile([P, T], U32, align_bytes=64)
        planes = keep.tile([P, T], U8, align_bytes=64)
        y = keep.tile([P, T], F32)
        banks = {}

        def loaded(t0, t1):
            for raw, (l0, l1) in zip(raws, LOADS):
                if l0 <= t0 and t1 <= l1:
                    return raw[:, :, t0 - l0 : t1 - l0].rearrange("p j t -> p t j")

        def by_vector(t0, t1):
            nc.vector.tensor_copy(grouped[:, t0:t1, :], loaded(t0, t1))

        def by_scalar(t0, t1):
            nc.scalar.copy(grouped[:, t0:t1, :], loaded(t0, t1))

        def project(t0, t1):
            nc.vector.quantize_mx(
                out=codes[:, t0:t1].bitcast(FP8X4),
                scales=planes[:, t0:t1],
                in_=grouped[:, t0:t1, :].rearrange("p t j -> p (t j)"),
            )
            acc = psum.tile([P, t1 - t0], F32, name=f"acc{t0}")
            nc.tensor.matmul_mx(
                out=acc[:],
                lhsT=w_codes[:].bitcast(FP8X4),
                lhsT_scale=w_plane[:],
                rhs=codes[:, t0:t1].bitcast(FP8X4),
                rhs_scale=planes[:, t0:t1],
                start=True,
                stop=True,
            )
            banks[t0] = acc

        def finish(t0, t1):
            nc.scalar.activation(y[:, t0:t1], banks[t0][:], RELU, bias=bias[:])

        by_vector(0, 304)
        by_scalar(304, 512)
        project(0, 256)
        project(256, 512)
        by_vector(512, 704)
        by_scalar(704, 768)
        finish(0, 256)
        by_vector(768, 832)
        project(512, 768)
        finish(256, 512)
        by_vector(832, 912)
        by_scalar(912, 1024)
        project(768, 896)
        project(896, 1024)
        finish(512, 768)
        finish(768, 896)
        finish(896, 1024)

        gate_of = [gates[0][:, 0, :], gates[1][:, 0, :], gates[1][:, 1, :]] + [gates[2][:, d, :] for d in range(3)]
        terms = [keep.tile([P, V], F32, name=f"term{d}") for d in range(D)]
        sums = [keep.tile([P, V], F32, name=f"sum{d}") for d in range(5)]

        def neighbour(d, v0=0, v1=V):
            idx = offsets[d][:, v0 // 16 : v1 // 16]
            nc.vector.tensor_tensor(terms[d][:, v0:v1], y[:].indirect(idx), gate_of[d][:, v0:v1], MULT)

        def add(dst, a, b_, v0=0, v1=V):
            nc.vector.tensor_tensor(dst[:, v0:v1], a[:, v0:v1], b_[:, v0:v1], ADD)

        neighbour(0)
        neighbour(1)
        neighbour(2)
        add(sums[0], terms[0], terms[1])
        neighbour(3)
        add(sums[1], sums[0], terms[2])
        neighbour(4)
        add(sums[2], sums[1], terms[3])
        neighbour(5, 0, HALF)
        add(sums[3], sums[2], terms[4])
        neighbour(5, HALF, V)
        add(sums[4], sums[3], terms[5], 0, HALF)
        nc.sync.dma_start(out=out[:, 0:HALF], in_=sums[4][:, 0:HALF])
        add(sums[4], sums[3], terms[5], HALF, V)
        nc.sync.dma_start(out=out[:, HALF:V], in_=sums[4][:, HALF:V])
